import numpy as np
import ml_dtypes


def mxq(x, axis, fmt="e4m3"):
    dtype, down = {"e4m3": (ml_dtypes.float8_e4m3fn, 7), "e5m2": (ml_dtypes.float8_e5m2, 14)}[fmt]
    v = np.moveaxis(np.asarray(x, np.float32).astype(ml_dtypes.bfloat16).astype(np.float64), axis, -1)
    blocks = v.reshape(v.shape[:-1] + (-1, 32))
    amax = np.abs(blocks).max(-1, keepdims=True)
    byte = np.maximum(np.where(amax > 0, np.frexp(amax)[1] - 1 + 127, 0) - down, 1)
    scale = np.exp2(byte - 127.0)
    codes = (blocks / scale).astype(np.float32).astype(dtype).astype(np.float64)
    return np.moveaxis((codes * scale).reshape(v.shape), -1, axis)


WIDE = False


def mx_kscale(k):
    if not WIDE:
        return np.ones(k)
    levels = np.array([10, -10, 5, -5, 0])
    if k % 512:
        return np.exp2(np.random.permutation(np.resize(levels, k // 32))).repeat(32)
    a = np.empty((k // 512, 16))
    for p in range(k // 512):
        a[p, :8] = np.random.permutation(np.resize(levels, 8))
        for g in range(8):
            far = levels[np.abs(levels - a[p, g]) >= 10]
            a[p, g + 8] = far[np.random.randint(len(far))]
    return np.exp2(a.ravel()).repeat(32)


def f64(x):
    return np.asarray(x).astype(np.float64)


def striped(idx):
    return np.tile(np.asarray(idx).reshape(-1, 16).T, (8, 1)).astype(np.uint16)


def unstriped(offs):
    return offs[:16].T.reshape(-1).astype(np.int64)


E2M1 = np.array([0.0, 0.5, 1.0, 1.5, 2.0, 3.0, 4.0, 6.0, -0.0, -0.5, -1.0, -1.5, -2.0, -3.0, -4.0, -6.0])


def pack_weight(w, fmt):
    k, n = w.shape
    w = f64(np.asarray(w, np.float32).astype(ml_dtypes.bfloat16)).reshape(k // 32, 32, n)
    amax = np.abs(w).max(1)
    if fmt == "e4m3":
        byte = np.frexp(amax)[1] - 1 + 127 - 7
    else:
        mant, ex = np.frexp(amax / 6.0)
        byte = np.where(mant > 0.5, ex, ex - 1) + 127
    byte = np.clip(np.where(amax > 0, byte, 1), 1, 254)
    scaled = (w * np.exp2(127.0 - byte)[:, None, :]).reshape(k, n).astype(np.float32)
    by_word = np.ascontiguousarray(scaled.reshape(k // 512, 128, 4, n).transpose(0, 1, 3, 2))
    if fmt == "e4m3":
        words = by_word.astype(ml_dtypes.float8_e4m3fn).view(np.uint8)
    else:
        c = by_word.astype(ml_dtypes.float4_e2m1fn).view(np.uint8) & 0xF
        words = (c[..., 0::2] | (c[..., 1::2] << 4)).reshape(k // 512, 128, 2 * n)
    return np.ascontiguousarray(words), np.ascontiguousarray(byte.astype(np.uint8).reshape(k // 512, 16, n))


def unpack_weight(words, scales, fmt):
    g, _, n = scales.shape
    words = np.ascontiguousarray(words).reshape(g, 128, n, -1)
    if fmt == "e4m3":
        vals = words.view(ml_dtypes.float8_e4m3fn).astype(np.float64)
    else:
        nib = np.empty((g, 128, n, 4), np.uint8)
        nib[..., 0::2] = words & 0xF
        nib[..., 1::2] = words >> 4
        vals = E2M1[nib]
    vals = vals * np.repeat(np.exp2(scales.astype(np.float64) - 127.0), 8, axis=1)[..., None]
    return vals.transpose(0, 1, 3, 2).reshape(g * 512, n)


D, E, T, I, Q = 512, 512, 2048, 512, 128


def setup_inputs():
    n = np.random.standard_normal
    idx = np.random.permutation(T)[:I]
    fd = mx_kscale(D)
    fe = mx_kscale(E)
    keysp = pack_weight(n((D, T)) / fd[:, None], "e2m1")
    valsp = pack_weight(n((E, T)) / fe[:, None], "e2m1")
    return {
        "query": (n((D, Q)) * 1.0 / np.sqrt(D) * fd[:, None]).astype(np.float32),
        "keys_words": keysp[0],
        "keys_scales": keysp[1],
        "aim": (np.random.uniform(0.5, 2.0, (Q, 1))).astype(np.float32),
        "soft": (np.random.uniform(0.5, 2.0, (Q, 1))).astype(np.float32),
        "gout": (n((E, Q)) * 1 / np.sqrt(E) * fe[:, None]).astype(np.float32),
        "vals_words": valsp[0],
        "vals_scales": valsp[1],
        "old": (0.5 * n((Q, T))).astype(np.float32),
        "offs": striped(idx),
    }


def reference(query, keys_words, keys_scales, aim, soft, gout, vals_words, vals_scales, old, offs):
    idx = unstriped(offs)
    keysu = unpack_weight(keys_words, keys_scales, "e2m1")
    valsu = unpack_weight(vals_words, vals_scales, "e2m1")
    queryq = mxq(f64(query), 0, "e4m3")
    keysidxg = keysu[:, idx]
    a = queryq.T @ keysidxg
    p = 1.0 / (np.square(f64(aim) - a) + f64(soft))
    z = np.sum(p, axis=1, keepdims=True)
    goutq = mxq(f64(gout), 0, "e4m3")
    valsidxg = valsu[:, idx]
    c0 = goutq.T @ valsidxg
    dz = np.sum(c0 * p / np.square(z) * (-1.0), axis=1, keepdims=True)
    dp = c0 / z + dz
    da = dp * (-1.0) / np.square(np.square(f64(aim) - a) + f64(soft)) * (f64(aim) - a) * 2.0 * (-1.0)
    gs = da * 512.0
    gf = np.zeros((Q, T))
    gf[:, idx] = gs
    y = f64(old) + gf
    return y

@@ -1,0 +1,157 @@
+from contextlib import ExitStack
+
+import concourse.mybir as mybir
+
+D, E, T, I, Q = 512, 512, 2048, 512, 128
+FLOPS = 2 * 2 * D * I * Q
+
+F32 = mybir.dt.float32
+BF16 = mybir.dt.bfloat16
+I32 = mybir.dt.int32
+U32 = mybir.dt.uint32
+U16 = mybir.dt.uint16
+U8 = mybir.dt.uint8
+FP8X4 = mybir.dt.float8_e4m3fn_x4
+FP4X4 = mybir.dt.float4_e2m1fn_x4
+ALU = mybir.AluOpType
+ACT = mybir.ActivationFunctionType
+
+P = 128
+H = 2
+NH = I // H
+OC = NH // 16
+OUT_CHUNKS = (256, 512, 512, 512, 256)
+
+
+def tile_attend_bnearpoint_s_kernel(tc, query, keys_words, keys_scales, aim, soft, gout, vals_words, vals_scales, old, offs, out):
+    nc = tc.nc
+    with ExitStack() as ctx:
+        sb = ctx.enter_context(tc.tile_pool(name="sb", bufs=1))
+        ps = ctx.enter_context(tc.psum_pool(name="ps", bufs=1))
+
+        def tile(name, shape, dt, tag=None):
+            return sb.tile(shape, dt, name=name, tag=tag or name, align_bytes=64)
+
+        offsets = tile("offsets", [P, I // 16], U16)
+        kw = tile("kw", [P, T], U16)
+        ks = tile("ks", [P, T], U8)
+        vs = tile("vs", [P, T], U8)
+        q_raw = tile("q_raw", [P, 4, Q], F32)
+        g_raw = tile("g_raw", [P, 4, Q], F32, tag="stage")
+        gf = tile("gf", [P, T], F32)
+        warm_in = tile("warm_in", [P, 1], F32, tag="aim")
+        warm_out = tile("warm_out", [P, 1], F32, tag="vw")
+        warm_sum = tile("warm_sum", [P, 1], F32, tag="soft")
+
+        def load_scales(dst, src):
+            for quad in range(4):
+                nc.sync.dma_start(out=dst[32 * quad : 32 * quad + 4, :].bitcast(I32), in_=src[0, 4 * quad : 4 * quad + 4, :].bitcast(I32))
+
+        nc.sync.dma_start(offsets[:], offs)
+        nc.scalar.dma_start(out=kw[:].bitcast(I32), in_=keys_words[0].bitcast(I32))
+        nc.scalar.dma_start(out=q_raw[:], in_=query.rearrange("(p j) w -> p j w", j=4))
+        nc.scalar.dma_start(out=g_raw[:], in_=gout.rearrange("(p j) w -> p j w", j=4))
+        nc.vector.memset(ks[:].bitcast(I32), 0)
+        nc.vector.memset(warm_in[:], 1.0)
+        nc.vector.memset(gf[:], 0.0)
+        nc.vector.memset(vs[:].bitcast(I32), 0)
+        nc.scalar.activation(warm_out[:], warm_in[:], ACT.Abs_reciprocal_sqrt, accum_out=warm_sum[:])
+        load_scales(ks, keys_scales)
+        vw = tile("vw", [P, T], U16, tag="vw")
+        aim_t = tile("aim_t", [P, 1], F32, tag="aim")
+        soft_t = tile("soft_t", [P, 1], F32, tag="soft")
+        nc.scalar.dma_start(out=vw[:].bitcast(I32), in_=vals_words[0].bitcast(I32))
+        nc.scalar.dma_start(out=aim_t[:], in_=aim)
+        nc.scalar.dma_start(out=soft_t[:], in_=soft)
+        load_scales(vs, vals_scales)
+
+        def interleave(name, raw):
+            grouped = tile(name + "_grp", [P, Q, 4], BF16)
+            nc.scalar.copy(grouped[:], raw[:].rearrange("p j w -> p w j"))
+            return grouped
+
+        def quantize(name, grouped):
+            codes = tile(name + "_codes", [P, Q], U32)
+            scales = tile(name + "_scales", [P, Q], U8)
+            nc.vector.quantize_mx(out=codes[:].bitcast(FP8X4), scales=scales[:], in_=grouped[:].rearrange("p w j -> p (w j)"))
+            return codes, scales
+
+        def gather(name, window, h, dt):
+            dst = tile("%s_g%d" % (name, h), [P, NH], dt)
+            nc.vector.tensor_copy(dst[:], window[:].indirect(offsets[:, h * OC : (h + 1) * OC]))
+            return dst[:]
+
+        def gather_all(name, window, dt, tag=None):
+            dst = tile("%s_g" % name, [P, I], dt, tag=tag)
+            nc.vector.tensor_copy(dst[:], window[:].indirect(offsets[:]))
+            return [dst[:, h * NH : (h + 1) * NH] for h in range(H)]
+
+        def product(name, h, stat, words, scales):
+            acc = ps.tile([P, NH], F32, name="%s%d" % (name, h))
+            nc.tensor.matmul_mx(out=acc[:], lhsT=stat[0][:].bitcast(FP8X4), lhsT_scale=stat[1][:],
+                                rhs=words.bitcast(FP4X4), rhs_scale=scales, start=True, stop=True)
+            return acc
+
+        def col(name):
+            return tile(name, [P, 1], F32)
+
+        q_grp = interleave("q", q_raw)
+        a_ps, p_t, p2_t, z_t = [], [], [], []
+        kw_g = gather_all("kw", kw, U16)
+        q_mx = quantize("q", q_grp)
+        for h in range(H):
+            ks_g = gather("ks", ks, h, U8)
+            a_ps.append(product("a", h, q_mx, kw_g[h], ks_g))
+        g_grp = interleave("g", g_raw)
+        old_t = tile("old_t", [P, T], F32, tag="stage")
+        nc.sync.dma_start(out=old_t[:], in_=old)
+        for h in range(H):
+            s = tile("s%d" % h, [P, NH], F32)
+            r = tile("r%d" % h, [P, NH], F32)
+            p = tile("p%d" % h, [P, NH], F32)
+            z = col("z%d" % h)
+            nc.scalar.activation(s[:], a_ps[h][:], ACT.Square, bias=aim_t[:], scale=-1.0)
+            nc.scalar.activation(r[:], s[:], ACT.Abs_reciprocal_sqrt, bias=soft_t[:])
+            nc.scalar.activation(p[:], r[:], ACT.Square, accum_out=z[:])
+            p_t.append(p)
+            z_t.append(z)
+        rz, alpha = col("rz"), col("alpha")
+        nc.scalar.activation(rz[:], z_t[0][:], ACT.Abs_reciprocal_sqrt, bias=z_t[1][:])
+        nc.scalar.activation(alpha[:], rz[:], ACT.Square, scale=32.0)
+        for h in range(H):
+            p2 = tile("p2%d" % h, [P, NH], F32)
+            nc.scalar.activation(p2[:], p_t[h][:], ACT.Square, scale=rz[:])
+            p2_t.append(p2)
+
+        vw_g = gather_all("vw", vw, U16, tag="ks_g0")
+        g_mx = quantize("g", g_grp)
+        c_ps = []
+        for h in range(H):
+            vs_g = gather("vs", vs, h, U8)
+            c_ps.append(product("c", h, g_mx, vw_g[h], vs_g))
+
+        beta_h = []
+        for h in range(H):
+            junk = tile("cp%d" % h, [P, NH], F32)
+            b = col("beta%d" % h)
+            nc.vector.scalar_tensor_tensor(junk[:], c_ps[h][:], alpha[:], p_t[h][:], ALU.mult, ALU.mult, accum_out=b[:])
+            beta_h.append(b)
+        beta = col("beta")
+        nc.scalar.activation(beta[:], beta_h[0][:], ACT.Identity, bias=beta_h[1][:])
+        x_t, y_t = [], []
+        for h in range(H):
+            y = tile("y%d" % h, [P, NH], F32)
+            nc.vector.scalar_tensor_tensor(y[:], a_ps[h][:], aim_t[:], p2_t[h][:], ALU.subtract, ALU.mult)
+            x = tile("x%d" % h, [P, NH], F32)
+            nc.scalar.activation(x[:], c_ps[h][:], ACT.Identity, bias=beta[:], scale=-1024.0)
+            x_t.append(x)
+            y_t.append(y)
+        for h in range(H):
+            nc.vector.tensor_tensor(gf[:].indirect(offsets[:, h * OC : (h + 1) * OC]), x_t[h][:], y_t[h][:], ALU.mult)
+
+        c0 = 0
+        for n, w in enumerate(OUT_CHUNKS):
+            res = tile("res%d" % n, [P, w], F32)
+            nc.vector.tensor_tensor(res[:], gf[:, c0 : c0 + w], old_t[:, c0 : c0 + w], ALU.add)
+            nc.sync.dma_start(out=out[:, c0 : c0 + w], in_=res[:])
+            c0 += w

@@ -37,32 +37,35 @@ def tile_attend_bnearpoint_s_kernel(tc, query, keys_words, keys_scales, aim, sof
         ks = tile("ks", [P, T], U8)
         vs = tile("vs", [P, T], U8)
         q_raw = tile("q_raw", [P, 4, Q], F32)
-        g_raw = tile("g_raw", [P, 4, Q], F32, tag="stage")
         gf = tile("gf", [P, T], F32)
-        warm_in = tile("warm_in", [P, 1], F32, tag="aim")
-        warm_out = tile("warm_out", [P, 1], F32, tag="vw")
-        warm_sum = tile("warm_sum", [P, 1], F32, tag="soft")
+        warm_in = tile("warm_in", [P, 1], F32, tag="g_raw")
+        warm_bias = tile("warm_bias", [P, 1], F32, tag="vw")
+        warm_out = tile("warm_out", [P, 1], F32, tag="aim_t")
+        warm_sum = tile("warm_sum", [P, 1], F32, tag="soft_t")
 
         def load_scales(dst, src):
             for quad in range(4):
                 nc.sync.dma_start(out=dst[32 * quad : 32 * quad + 4, :].bitcast(I32), in_=src[0, 4 * quad : 4 * quad + 4, :].bitcast(I32))
 
         nc.sync.dma_start(offsets[:], offs)
-        nc.scalar.dma_start(out=kw[:].bitcast(I32), in_=keys_words[0].bitcast(I32))
-        nc.scalar.dma_start(out=q_raw[:], in_=query.rearrange("(p j) w -> p j w", j=4))
-        nc.scalar.dma_start(out=g_raw[:], in_=gout.rearrange("(p j) w -> p j w", j=4))
+        nc.sync.dma_start(out=kw[:].bitcast(I32), in_=keys_words[0].bitcast(I32))
+        nc.sync.dma_start(out=q_raw[:], in_=query.rearrange("(p j) w -> p j w", j=4))
         nc.vector.memset(ks[:].bitcast(I32), 0)
-        nc.vector.memset(warm_in[:], 1.0)
-        nc.vector.memset(gf[:], 0.0)
-        nc.vector.memset(vs[:].bitcast(I32), 0)
-        nc.scalar.activation(warm_out[:], warm_in[:], ACT.Abs_reciprocal_sqrt, accum_out=warm_sum[:])
         load_scales(ks, keys_scales)
-        vw = tile("vw", [P, T], U16, tag="vw")
-        aim_t = tile("aim_t", [P, 1], F32, tag="aim")
-        soft_t = tile("soft_t", [P, 1], F32, tag="soft")
-        nc.scalar.dma_start(out=vw[:].bitcast(I32), in_=vals_words[0].bitcast(I32))
-        nc.scalar.dma_start(out=aim_t[:], in_=aim)
-        nc.scalar.dma_start(out=soft_t[:], in_=soft)
+        nc.vector.memset(gf[:, : T // 2], 0.0)
+        nc.vector.memset(warm_in[:], 1.0)
+        nc.vector.memset(warm_bias[:], 0.0)
+        nc.vector.memset(gf[:, T // 2 :], 0.0)
+        nc.vector.memset(vs[:].bitcast(I32), 0)
+        nc.scalar.activation(warm_out[:], warm_in[:], ACT.Abs_reciprocal_sqrt, bias=warm_bias[:], accum_out=warm_sum[:])
+        g_raw = tile("g_raw", [P, 4, Q], F32)
+        vw = tile("vw", [P, T], U16)
+        aim_t = tile("aim_t", [P, 1], F32)
+        soft_t = tile("soft_t", [P, 1], F32)
+        nc.sync.dma_start(out=g_raw[:], in_=gout.rearrange("(p j) w -> p j w", j=4))
+        nc.sync.dma_start(out=vw[:].bitcast(I32), in_=vals_words[0].bitcast(I32))
+        nc.sync.dma_start(out=aim_t[:], in_=aim)
+        nc.sync.dma_start(out=soft_t[:], in_=soft)
         load_scales(vs, vals_scales)
 
         def interleave(name, raw):
@@ -70,14 +73,14 @@ def tile_attend_bnearpoint_s_kernel(tc, query, keys_words, keys_scales, aim, sof
             nc.scalar.copy(grouped[:], raw[:].rearrange("p j w -> p w j"))
             return grouped
 
-        def quantize(name, grouped):
+        def quantize(name, grouped, tag=None):
             codes = tile(name + "_codes", [P, Q], U32)
-            scales = tile(name + "_scales", [P, Q], U8)
+            scales = tile(name + "_scales", [P, Q], U8, tag=tag)
             nc.vector.quantize_mx(out=codes[:].bitcast(FP8X4), scales=scales[:], in_=grouped[:].rearrange("p w j -> p (w j)"))
             return codes, scales
 
-        def gather(name, window, h, dt):
-            dst = tile("%s_g%d" % (name, h), [P, NH], dt)
+        def gather(name, window, h, dt, tag=None):
+            dst = tile("%s_g%d" % (name, h), [P, NH], dt, tag=tag)
             nc.vector.tensor_copy(dst[:], window[:].indirect(offsets[:, h * OC : (h + 1) * OC]))
             return dst[:]
 
@@ -103,10 +106,8 @@ def tile_attend_bnearpoint_s_kernel(tc, query, keys_words, keys_scales, aim, sof
             ks_g = gather("ks", ks, h, U8)
             a_ps.append(product("a", h, q_mx, kw_g[h], ks_g))
         g_grp = interleave("g", g_raw)
-        old_t = tile("old_t", [P, T], F32, tag="stage")
-        nc.sync.dma_start(out=old_t[:], in_=old)
         for h in range(H):
-            s = tile("s%d" % h, [P, NH], F32)
+            s = tile("s%d" % h, [P, NH], F32, tag=("g_raw", None)[h])
             r = tile("r%d" % h, [P, NH], F32)
             p = tile("p%d" % h, [P, NH], F32)
             z = col("z%d" % h)
@@ -124,10 +125,12 @@ def tile_attend_bnearpoint_s_kernel(tc, query, keys_words, keys_scales, aim, sof
             p2_t.append(p2)
 
         vw_g = gather_all("vw", vw, U16, tag="ks_g0")
-        g_mx = quantize("g", g_grp)
+        old_t = tile("old_t", [P, T], F32, tag="vw")
+        nc.sync.dma_start(out=old_t[:], in_=old)
+        g_mx = quantize("g", g_grp, tag="ks_g1")
         c_ps = []
         for h in range(H):
-            vs_g = gather("vs", vs, h, U8)
+            vs_g = gather("vs", vs, h, U8, tag=("kw_g", "q_codes")[h])
             c_ps.append(product("c", h, g_mx, vw_g[h], vs_g))
 
         beta_h = []

@@ -2,8 +2,8 @@ from contextlib import ExitStack
 
 import concourse.mybir as mybir
 
-D, E, T, I, Q = 512, 512, 2048, 512, 128
-FLOPS = 2 * 2 * D * I * Q
+D, T, SLOTS, Q = 512, 2048, 512, 128
+FLOPS = 2 * 2 * D * SLOTS * Q
 
 F32 = mybir.dt.float32
 BF16 = mybir.dt.bfloat16
@@ -17,13 +17,16 @@ ALU = mybir.AluOpType
 ACT = mybir.ActivationFunctionType
 
 P = 128
-H = 2
-NH = I // H
-OC = NH // 16
-OUT_CHUNKS = (256, 512, 512, 512, 256)
+PLACES = 4
+HALVES = 2
+HALF = SLOTS // HALVES
+HALF_COLS = HALF // 16
+STORE_WIDTHS = (128, 256, 256, 384, 512, 512)
 
 
-def tile_attend_bnearpoint_s_kernel(tc, query, keys_words, keys_scales, aim, soft, gout, vals_words, vals_scales, old, offs, out):
+def tile_attend_bnearpoint_s_kernel(
+    tc, query, keys_words, keys_scales, aim, soft, gout, vals_words, vals_scales, old, offs, out
+):
     nc = tc.nc
     with ExitStack() as ctx:
         sb = ctx.enter_context(tc.tile_pool(name="sb", bufs=1))
@@ -32,24 +35,69 @@ def tile_attend_bnearpoint_s_kernel(tc, query, keys_words, keys_scales, aim, sof
         def tile(name, shape, dt, tag=None):
             return sb.tile(shape, dt, name=name, tag=tag or name, align_bytes=64)
 
-        offsets = tile("offsets", [P, I // 16], U16)
+        def column(name, tag=None):
+            return tile(name, [P, 1], F32, tag=tag)
+
+        def half_offsets(h):
+            return offsets[:, h * HALF_COLS : (h + 1) * HALF_COLS]
+
+        def load_scales(dst, src):
+            for n in range(4):
+                nc.sync.dma_start(
+                    out=dst[32 * n : 32 * n + 4, :].bitcast(I32), in_=src[0, 4 * n : 4 * n + 4, :].bitcast(I32)
+                )
+
+        def interleave(name, raw):
+            grouped = tile(name + "_grp", [P, Q, PLACES], BF16)
+            nc.scalar.copy(grouped[:], raw[:].rearrange("p j w -> p w j"))
+            return grouped
+
+        def quantize(name, grouped):
+            codes = tile(name + "_codes", [P, Q], U32)
+            scales = tile(name + "_scales", [P, Q], U8)
+            nc.vector.quantize_mx(
+                out=codes[:].bitcast(FP8X4), scales=scales[:], in_=grouped[:].rearrange("p w j -> p (w j)")
+            )
+            return codes, scales
+
+        def gather_words(name, window):
+            dst = tile(name + "_g", [P, SLOTS], U16)
+            nc.vector.tensor_copy(dst[:], window[:].indirect(offsets[:]))
+            return [dst[:, h * HALF : (h + 1) * HALF] for h in range(HALVES)]
+
+        def gather_scales(name, window, h):
+            dst = tile("%s_g%d" % (name, h), [P, HALF], U8)
+            nc.vector.tensor_copy(dst[:], window[:].indirect(half_offsets(h)))
+            return dst[:]
+
+        def product(name, h, stationary, words, scales):
+            codes, code_scales = stationary
+            acc = ps.tile([P, HALF], F32, name="%s%d" % (name, h))
+            nc.tensor.matmul_mx(
+                out=acc[:],
+                lhsT=codes[:].bitcast(FP8X4),
+                lhsT_scale=code_scales[:],
+                rhs=words.bitcast(FP4X4),
+                rhs_scale=scales,
+                start=True,
+                stop=True,
+            )
+            return acc
+
+        offsets = tile("offsets", [P, SLOTS // 16], U16)
         kw = tile("kw", [P, T], U16)
         ks = tile("ks", [P, T], U8)
         vs = tile("vs", [P, T], U8)
-        q_raw = tile("q_raw", [P, 4, Q], F32)
+        q_raw = tile("q_raw", [P, PLACES, Q], F32)
         gf = tile("gf", [P, T], F32)
-        warm_in = tile("warm_in", [P, 1], F32, tag="g_raw")
-        warm_bias = tile("warm_bias", [P, 1], F32, tag="vw")
-        warm_out = tile("warm_out", [P, 1], F32, tag="aim_t")
-        warm_sum = tile("warm_sum", [P, 1], F32, tag="soft_t")
-
-        def load_scales(dst, src):
-            for quad in range(4):
-                nc.sync.dma_start(out=dst[32 * quad : 32 * quad + 4, :].bitcast(I32), in_=src[0, 4 * quad : 4 * quad + 4, :].bitcast(I32))
+        warm_in = column("warm_in", tag="g_raw")
+        warm_bias = column("warm_bias", tag="vw")
+        warm_out = column("warm_out", tag="aim_t")
+        warm_sum = column("warm_sum", tag="soft_t")
 
         nc.sync.dma_start(offsets[:], offs)
         nc.sync.dma_start(out=kw[:].bitcast(I32), in_=keys_words[0].bitcast(I32))
-        nc.sync.dma_start(out=q_raw[:], in_=query.rearrange("(p j) w -> p j w", j=4))
+        nc.sync.dma_start(out=q_raw[:], in_=query.rearrange("(p j) w -> p j w", j=PLACES))
         nc.vector.memset(ks[:].bitcast(I32), 0)
         load_scales(ks, keys_scales)
         nc.vector.memset(gf[:, : T // 2], 0.0)
@@ -57,104 +105,91 @@ def tile_attend_bnearpoint_s_kernel(tc, query, keys_words, keys_scales, aim, sof
         nc.vector.memset(warm_bias[:], 0.0)
         nc.vector.memset(gf[:, T // 2 :], 0.0)
         nc.vector.memset(vs[:].bitcast(I32), 0)
-        nc.scalar.activation(warm_out[:], warm_in[:], ACT.Abs_reciprocal_sqrt, bias=warm_bias[:], accum_out=warm_sum[:])
-        g_raw = tile("g_raw", [P, 4, Q], F32)
+        nc.scalar.activation(
+            warm_out[:], warm_in[:], ACT.Abs_reciprocal_sqrt, bias=warm_bias[:], accum_out=warm_sum[:]
+        )
+        g_raw = tile("g_raw", [P, PLACES, Q], F32)
         vw = tile("vw", [P, T], U16)
-        aim_t = tile("aim_t", [P, 1], F32)
-        soft_t = tile("soft_t", [P, 1], F32)
-        nc.sync.dma_start(out=g_raw[:], in_=gout.rearrange("(p j) w -> p j w", j=4))
+        aim_t = column("aim_t")
+        soft_t = column("soft_t")
+        nc.sync.dma_start(out=g_raw[:], in_=gout.rearrange("(p j) w -> p j w", j=PLACES))
         nc.sync.dma_start(out=vw[:].bitcast(I32), in_=vals_words[0].bitcast(I32))
         nc.sync.dma_start(out=aim_t[:], in_=aim)
         nc.sync.dma_start(out=soft_t[:], in_=soft)
         load_scales(vs, vals_scales)
 
-        def interleave(name, raw):
-            grouped = tile(name + "_grp", [P, Q, 4], BF16)
-            nc.scalar.copy(grouped[:], raw[:].rearrange("p j w -> p w j"))
-            return grouped
-
-        def quantize(name, grouped, tag=None):
-            codes = tile(name + "_codes", [P, Q], U32)
-            scales = tile(name + "_scales", [P, Q], U8, tag=tag)
-            nc.vector.quantize_mx(out=codes[:].bitcast(FP8X4), scales=scales[:], in_=grouped[:].rearrange("p w j -> p (w j)"))
-            return codes, scales
-
-        def gather(name, window, h, dt, tag=None):
-            dst = tile("%s_g%d" % (name, h), [P, NH], dt, tag=tag)
-            nc.vector.tensor_copy(dst[:], window[:].indirect(offsets[:, h * OC : (h + 1) * OC]))
-            return dst[:]
-
-        def gather_all(name, window, dt, tag=None):
-            dst = tile("%s_g" % name, [P, I], dt, tag=tag)
-            nc.vector.tensor_copy(dst[:], window[:].indirect(offsets[:]))
-            return [dst[:, h * NH : (h + 1) * NH] for h in range(H)]
-
-        def product(name, h, stat, words, scales):
-            acc = ps.tile([P, NH], F32, name="%s%d" % (name, h))
-            nc.tensor.matmul_mx(out=acc[:], lhsT=stat[0][:].bitcast(FP8X4), lhsT_scale=stat[1][:],
-                                rhs=words.bitcast(FP4X4), rhs_scale=scales, start=True, stop=True)
-            return acc
-
-        def col(name):
-            return tile(name, [P, 1], F32)
-
         q_grp = interleave("q", q_raw)
-        a_ps, p_t, p2_t, z_t = [], [], [], []
-        kw_g = gather_all("kw", kw, U16)
+        kw_g = gather_words("kw", kw)
         q_mx = quantize("q", q_grp)
-        for h in range(H):
-            ks_g = gather("ks", ks, h, U8)
-            a_ps.append(product("a", h, q_mx, kw_g[h], ks_g))
+        a_ps = [product("a", h, q_mx, kw_g[h], gather_scales("ks", ks, h)) for h in range(HALVES)]
         g_grp = interleave("g", g_raw)
-        for h in range(H):
-            s = tile("s%d" % h, [P, NH], F32, tag=("g_raw", None)[h])
-            r = tile("r%d" % h, [P, NH], F32)
-            p = tile("p%d" % h, [P, NH], F32)
-            z = col("z%d" % h)
+        p_t, z_t = [], []
+        for h in range(HALVES):
+            s = tile("s%d" % h, [P, HALF], F32, tag=("g_raw", None)[h])
+            r = tile("r%d" % h, [P, HALF], F32)
+            p = tile("p%d" % h, [P, HALF], F32)
+            z = column("z%d" % h)
             nc.scalar.activation(s[:], a_ps[h][:], ACT.Square, bias=aim_t[:], scale=-1.0)
             nc.scalar.activation(r[:], s[:], ACT.Abs_reciprocal_sqrt, bias=soft_t[:])
             nc.scalar.activation(p[:], r[:], ACT.Square, accum_out=z[:])
             p_t.append(p)
             z_t.append(z)
-        rz, alpha = col("rz"), col("alpha")
-        nc.scalar.activation(rz[:], z_t[0][:], ACT.Abs_reciprocal_sqrt, bias=z_t[1][:])
-        nc.scalar.activation(alpha[:], rz[:], ACT.Square, scale=32.0)
-        for h in range(H):
-            p2 = tile("p2%d" % h, [P, NH], F32)
-            nc.scalar.activation(p2[:], p_t[h][:], ACT.Square, scale=rz[:])
-            p2_t.append(p2)
 
-        vw_g = gather_all("vw", vw, U16, tag="ks_g0")
+        vw_g = gather_words("vw", vw)
+        vs_g0 = gather_scales("vs", vs, 0)
+        g_mx = quantize("g", g_grp)
+        c_ps = [product("c", 0, g_mx, vw_g[0], vs_g0)]
+        c_ps.append(product("c", 1, g_mx, vw_g[1], gather_scales("vs", vs, 1)))
         old_t = tile("old_t", [P, T], F32, tag="vw")
         nc.sync.dma_start(out=old_t[:], in_=old)
-        g_mx = quantize("g", g_grp, tag="ks_g1")
-        c_ps = []
-        for h in range(H):
-            vs_g = gather("vs", vs, h, U8, tag=("kw_g", "q_codes")[h])
-            c_ps.append(product("c", h, g_mx, vw_g[h], vs_g))
 
-        beta_h = []
-        for h in range(H):
-            junk = tile("cp%d" % h, [P, NH], F32)
-            b = col("beta%d" % h)
-            nc.vector.scalar_tensor_tensor(junk[:], c_ps[h][:], alpha[:], p_t[h][:], ALU.mult, ALU.mult, accum_out=b[:])
-            beta_h.append(b)
-        beta = col("beta")
-        nc.scalar.activation(beta[:], beta_h[0][:], ACT.Identity, bias=beta_h[1][:])
-        x_t, y_t = [], []
-        for h in range(H):
-            y = tile("y%d" % h, [P, NH], F32)
-            nc.vector.scalar_tensor_tensor(y[:], a_ps[h][:], aim_t[:], p2_t[h][:], ALU.subtract, ALU.mult)
-            x = tile("x%d" % h, [P, NH], F32)
-            nc.scalar.activation(x[:], c_ps[h][:], ACT.Identity, bias=beta[:], scale=-1024.0)
-            x_t.append(x)
-            y_t.append(y)
-        for h in range(H):
-            nc.vector.tensor_tensor(gf[:].indirect(offsets[:, h * OC : (h + 1) * OC]), x_t[h][:], y_t[h][:], ALU.mult)
+        neg_t = [column("neg_t%d" % h) for h in range(HALVES)]
+        x_t = [tile("x%d" % h, [P, HALF], F32) for h in range(HALVES)]
+        y_t = [tile("y%d" % h, [P, HALF], F32, tag=("vs", "vs_g0")[h]) for h in range(HALVES)]
 
-        c0 = 0
-        for n, w in enumerate(OUT_CHUNKS):
-            res = tile("res%d" % n, [P, w], F32)
-            nc.vector.tensor_tensor(res[:], gf[:, c0 : c0 + w], old_t[:, c0 : c0 + w], ALU.add)
-            nc.sync.dma_start(out=out[:, c0 : c0 + w], in_=res[:])
-            c0 += w
+        def sum_neg_cp(h):
+            terms = tile("cp%d" % h, [P, HALF], F32)
+            nc.vector.scalar_tensor_tensor(
+                terms[:], c_ps[h][:], -1.0, p_t[h][:], ALU.mult, ALU.mult, accum_out=neg_t[h][:]
+            )
+
+        def square_p(h):
+            p2 = tile("p2%d" % h, [P, HALF], F32)
+            nc.scalar.activation(p2[:], p_t[h][:], ACT.Square)
+            return p2
+
+        def make_y(h, p2):
+            nc.vector.scalar_tensor_tensor(y_t[h][:], a_ps[h][:], aim_t[:], p2[:], ALU.subtract, ALU.mult)
+
+        z_sum = column("z_sum")
+        sum_neg_cp(0)
+        p2_first = square_p(0)
+        nc.scalar.activation(z_sum[:], z_t[0][:], ACT.Identity, bias=z_t[1][:])
+        zc_first = tile("zc_first", [P, HALF], F32)
+        nc.scalar.activation(zc_first[:], c_ps[0][:], ACT.Copy, scale=z_sum[:])
+        p2_second = square_p(1)
+        make_y(0, p2_first)
+        sum_neg_cp(1)
+        nc.vector.tensor_scalar(x_t[0][:], zc_first[:], neg_t[0][:], neg_t[1][:], ALU.add, ALU.add)
+        make_y(1, p2_second)
+        neg_t_sum = column("neg_t_sum")
+        nc.scalar.activation(neg_t_sum[:], neg_t[0][:], ACT.Identity, bias=neg_t[1][:])
+        nc.scalar.activation(x_t[1][:], c_ps[1][:], ACT.Identity, bias=neg_t_sum[:], scale=z_sum[:])
+
+        inv_root_z = column("inv_root_z", tag="zc_first")
+        inv_z, factor, neg_factor = column("inv_z"), column("factor"), column("neg_factor")
+        nc.scalar.activation(inv_root_z[:], z_sum[:], ACT.Abs_reciprocal_sqrt)
+        nc.scalar.activation(inv_z[:], inv_root_z[:], ACT.Square)
+        nc.scalar.activation(factor[:], inv_z[:], ACT.Square, scale=32.0)
+        nc.scalar.activation(neg_factor[:], factor[:], ACT.Copy, scale=-1.0)
+
+        for h in range(HALVES):
+            nc.vector.tensor_tensor(gf[:].indirect(half_offsets(h)), x_t[h][:], y_t[h][:], ALU.mult)
+
+        start = 0
+        for n, width in enumerate(STORE_WIDTHS):
+            cols = slice(start, start + width)
+            res = tile("res%d" % n, [P, width], F32)
+            nc.vector.scalar_tensor_tensor(res[:], gf[:, cols], neg_factor[:], old_t[:, cols], ALU.mult, ALU.add)
+            nc.sync.dma_start(out=out[:, cols], in_=res[:])
+            start += width

from contextlib import ExitStack

import concourse.mybir as mybir

D, T, SLOTS, Q = 512, 2048, 512, 128
FLOPS = 2 * 2 * D * SLOTS * Q

F32 = mybir.dt.float32
BF16 = mybir.dt.bfloat16
I32 = mybir.dt.int32
U32 = mybir.dt.uint32
U16 = mybir.dt.uint16
U8 = mybir.dt.uint8
FP8X4 = mybir.dt.float8_e4m3fn_x4
FP4X4 = mybir.dt.float4_e2m1fn_x4
ALU = mybir.AluOpType
ACT = mybir.ActivationFunctionType

P = 128
PLACES = 4
HALVES = 2
HALF = SLOTS // HALVES
HALF_COLS = HALF // 16
STORE_WIDTHS = (128, 256, 256, 384, 512, 512)


def tile_attend_bnearpoint_s_kernel(
    tc, query, keys_words, keys_scales, aim, soft, gout, vals_words, vals_scales, old, offs, out
):
    nc = tc.nc
    with ExitStack() as ctx:
        sb = ctx.enter_context(tc.tile_pool(name="sb", bufs=1))
        ps = ctx.enter_context(tc.psum_pool(name="ps", bufs=1))

        def tile(name, shape, dt, tag=None):
            return sb.tile(shape, dt, name=name, tag=tag or name, align_bytes=64)

        def column(name, tag=None):
            return tile(name, [P, 1], F32, tag=tag)

        def half_offsets(h):
            return offsets[:, h * HALF_COLS : (h + 1) * HALF_COLS]

        def load_scales(dst, src):
            for n in range(4):
                nc.sync.dma_start(
                    out=dst[32 * n : 32 * n + 4, :].bitcast(I32), in_=src[0, 4 * n : 4 * n + 4, :].bitcast(I32)
                )

        def interleave(name, raw):
            grouped = tile(name + "_grp", [P, Q, PLACES], BF16)
            nc.scalar.copy(grouped[:], raw[:].rearrange("p j w -> p w j"))
            return grouped

        def quantize(name, grouped):
            codes = tile(name + "_codes", [P, Q], U32)
            scales = tile(name + "_scales", [P, Q], U8)
            nc.vector.quantize_mx(
                out=codes[:].bitcast(FP8X4), scales=scales[:], in_=grouped[:].rearrange("p w j -> p (w j)")
            )
            return codes, scales

        def gather_words(name, window):
            dst = tile(name + "_g", [P, SLOTS], U16)
            nc.vector.tensor_copy(dst[:], window[:].indirect(offsets[:]))
            return [dst[:, h * HALF : (h + 1) * HALF] for h in range(HALVES)]

        def gather_scales(name, window, h):
            dst = tile("%s_g%d" % (name, h), [P, HALF], U8)
            nc.vector.tensor_copy(dst[:], window[:].indirect(half_offsets(h)))
            return dst[:]

        def product(name, h, stationary, words, scales):
            codes, code_scales = stationary
            acc = ps.tile([P, HALF], F32, name="%s%d" % (name, h))
            nc.tensor.matmul_mx(
                out=acc[:],
                lhsT=codes[:].bitcast(FP8X4),
                lhsT_scale=code_scales[:],
                rhs=words.bitcast(FP4X4),
                rhs_scale=scales,
                start=True,
                stop=True,
            )
            return acc

        offsets = tile("offsets", [P, SLOTS // 16], U16)
        kw = tile("kw", [P, T], U16)
        ks = tile("ks", [P, T], U8)
        vs = tile("vs", [P, T], U8)
        q_raw = tile("q_raw", [P, PLACES, Q], F32)
        gf = tile("gf", [P, T], F32)
        warm_in = column("warm_in", tag="g_raw")
        warm_bias = column("warm_bias", tag="vw")
        warm_out = column("warm_out", tag="aim_t")
        warm_sum = column("warm_sum", tag="soft_t")

        nc.sync.dma_start(offsets[:], offs)
        nc.sync.dma_start(out=kw[:].bitcast(I32), in_=keys_words[0].bitcast(I32))
        nc.sync.dma_start(out=q_raw[:], in_=query.rearrange("(p j) w -> p j w", j=PLACES))
        nc.vector.memset(ks[:].bitcast(I32), 0)
        load_scales(ks, keys_scales)
        nc.vector.memset(gf[:, : T // 2], 0.0)
        nc.vector.memset(warm_in[:], 1.0)
        nc.vector.memset(warm_bias[:], 0.0)
        nc.vector.memset(gf[:, T // 2 :], 0.0)
        nc.vector.memset(vs[:].bitcast(I32), 0)
        nc.scalar.activation(
            warm_out[:], warm_in[:], ACT.Abs_reciprocal_sqrt, bias=warm_bias[:], accum_out=warm_sum[:]
        )
        g_raw = tile("g_raw", [P, PLACES, Q], F32)
        vw = tile("vw", [P, T], U16)
        aim_t = column("aim_t")
        soft_t = column("soft_t")
        nc.sync.dma_start(out=g_raw[:], in_=gout.rearrange("(p j) w -> p j w", j=PLACES))
        nc.sync.dma_start(out=vw[:].bitcast(I32), in_=vals_words[0].bitcast(I32))
        nc.sync.dma_start(out=aim_t[:], in_=aim)
        nc.sync.dma_start(out=soft_t[:], in_=soft)
        load_scales(vs, vals_scales)

        q_grp = interleave("q", q_raw)
        kw_g = gather_words("kw", kw)
        q_mx = quantize("q", q_grp)
        a_ps = [product("a", h, q_mx, kw_g[h], gather_scales("ks", ks, h)) for h in range(HALVES)]
        g_grp = interleave("g", g_raw)
        p_t, z_t = [], []
        for h in range(HALVES):
            s = tile("s%d" % h, [P, HALF], F32, tag=("g_raw", None)[h])
            r = tile("r%d" % h, [P, HALF], F32)
            p = tile("p%d" % h, [P, HALF], F32)
            z = column("z%d" % h)
            nc.scalar.activation(s[:], a_ps[h][:], ACT.Square, bias=aim_t[:], scale=-1.0)
            nc.scalar.activation(r[:], s[:], ACT.Abs_reciprocal_sqrt, bias=soft_t[:])
            nc.scalar.activation(p[:], r[:], ACT.Square, accum_out=z[:])
            p_t.append(p)
            z_t.append(z)

        vw_g = gather_words("vw", vw)
        vs_g0 = gather_scales("vs", vs, 0)
        g_mx = quantize("g", g_grp)
        c_ps = [product("c", 0, g_mx, vw_g[0], vs_g0)]
        c_ps.append(product("c", 1, g_mx, vw_g[1], gather_scales("vs", vs, 1)))
        old_t = tile("old_t", [P, T], F32, tag="vw")
        nc.sync.dma_start(out=old_t[:], in_=old)

        neg_t = [column("neg_t%d" % h) for h in range(HALVES)]
        x_t = [tile("x%d" % h, [P, HALF], F32) for h in range(HALVES)]
        y_t = [tile("y%d" % h, [P, HALF], F32, tag=("vs", "vs_g0")[h]) for h in range(HALVES)]

        def sum_neg_cp(h):
            terms = tile("cp%d" % h, [P, HALF], F32)
            nc.vector.scalar_tensor_tensor(
                terms[:], c_ps[h][:], -1.0, p_t[h][:], ALU.mult, ALU.mult, accum_out=neg_t[h][:]
            )

        def square_p(h):
            p2 = tile("p2%d" % h, [P, HALF], F32)
            nc.scalar.activation(p2[:], p_t[h][:], ACT.Square)
            return p2

        def make_y(h, p2):
            nc.vector.scalar_tensor_tensor(y_t[h][:], a_ps[h][:], aim_t[:], p2[:], ALU.subtract, ALU.mult)

        z_sum = column("z_sum")
        sum_neg_cp(0)
        p2_first = square_p(0)
        nc.scalar.activation(z_sum[:], z_t[0][:], ACT.Identity, bias=z_t[1][:])
        zc_first = tile("zc_first", [P, HALF], F32)
        nc.scalar.activation(zc_first[:], c_ps[0][:], ACT.Copy, scale=z_sum[:])
        p2_second = square_p(1)
        make_y(0, p2_first)
        sum_neg_cp(1)
        nc.vector.tensor_scalar(x_t[0][:], zc_first[:], neg_t[0][:], neg_t[1][:], ALU.add, ALU.add)
        make_y(1, p2_second)
        neg_t_sum = column("neg_t_sum")
        nc.scalar.activation(neg_t_sum[:], neg_t[0][:], ACT.Identity, bias=neg_t[1][:])
        nc.scalar.activation(x_t[1][:], c_ps[1][:], ACT.Identity, bias=neg_t_sum[:], scale=z_sum[:])

        inv_root_z = column("inv_root_z", tag="zc_first")
        inv_z, factor, neg_factor = column("inv_z"), column("factor"), column("neg_factor")
        nc.scalar.activation(inv_root_z[:], z_sum[:], ACT.Abs_reciprocal_sqrt)
        nc.scalar.activation(inv_z[:], inv_root_z[:], ACT.Square)
        nc.scalar.activation(factor[:], inv_z[:], ACT.Square, scale=32.0)
        nc.scalar.activation(neg_factor[:], factor[:], ACT.Copy, scale=-1.0)

        for h in range(HALVES):
            nc.vector.tensor_tensor(gf[:].indirect(half_offsets(h)), x_t[h][:], y_t[h][:], ALU.mult)

        start = 0
        for n, width in enumerate(STORE_WIDTHS):
            cols = slice(start, start + width)
            res = tile("res%d" % n, [P, width], F32)
            nc.vector.scalar_tensor_tensor(res[:], gf[:, cols], neg_factor[:], old_t[:, cols], ALU.mult, ALU.add)
            nc.sync.dma_start(out=out[:, cols], in_=res[:])
            start += width
